import numpy as np
CORES = [64,65,66,67,68,69,70,71,72,73,74,75,76,77,78,79,80,81,82,83,84,85,86,87,88,89,90,91,92,93,94,95]
N = 32
ROWS, COLS = 8, 4
def setup_inputs(rng):
    return {"x": rng.standard_normal((N, 128, 256), dtype=np.float32)}
def reference(x):
    g = x.astype(np.float64).reshape(ROWS, COLS, 128, 256)
    rs = g.sum(axis=1)
    cs = g.sum(axis=0)
    y1 = np.stack([rs[r // COLS] for r in range(N)]).astype(x.dtype)
    y2 = np.stack([cs[r % COLS] for r in range(N)]).astype(x.dtype)
    return {"y1": y1, "y2": y2}

@@ -1,0 +1,126 @@
+from concourse.bass import DstId, RemoteDMATransfer
+import comms_topo
+
+SCRATCH = {
+    "xs": ("dram", [4, 128, 64], "float32"),
+    "rowin": ("dram", [4, 128, 64], "float32"),
+    "r1": ("dram", [4, 128, 64], "float32"),
+    "cin": ("dram", [8, 128, 64], "float32"),
+    "r2": ("dram", [4, 128, 64], "float32"),
+}
+SEMAPHORES = ["ld", "st1", "st2", "sent", "semR", "semP", "semS", "semO", "r1", "c0", "c1", "c2", "c3"]
+
+FIRST_CHIP = 8
+OMAP = {0: 6, 1: 7, 2: 3, 3: 2}
+SMAP = {0: 0, 1: 1, 2: 4, 3: 5}
+PMAP = {0: 6, 1: 7, 2: 2, 3: 3}
+
+
+def inv(m, j):
+    for k in m:
+        if m[k] == j:
+            return k
+    return None
+
+
+def prim_mate(k):
+    return k + 4 * (k % 2)
+
+
+def bits(n, at):
+    return ((1 << n) - 1) << at
+
+
+def plan(core):
+    chip, j = divmod(core, 8)
+    ci = chip - FIRST_CHIP
+    k, h = j % 4, j // 4
+
+    def at(c, jj):
+        return (FIRST_CHIP + c) * 8 + jj
+
+    def own(kk, q, slot0):
+        return [("xs", q) if kk + 4 * hh == j else ("cin", slot0 + hh) for hh in (0, 1)]
+
+    calls = []
+    tr = []
+    for t in range(4):
+        tr.append(([("xs", t)], [(at(ci, 4 * (1 - h) + t), "rowin", k)], "semR"))
+    tr.append(([("xs", ci)], [(at(ci, OMAP[k]), "cin", h)], "semO"))
+    if SMAP[k] != j:
+        tr.append(([("xs", ci ^ 2)], [(at(ci, SMAP[k]), "cin", h)], "semS"))
+    if PMAP[k] != j:
+        tr.append(([("xs", ci ^ 1)], [(at(ci, PMAP[k]), "cin", 4 + h)], "semP"))
+        tr.append(([("xs", ci ^ 3)], [(at(ci, PMAP[k]), "cin", 6 + h)], "semP"))
+    calls.append(([], [t + (bits(2, 2 * i),) for i, t in enumerate(tr)]))
+    kp = inv(PMAP, j)
+    if kp is not None:
+        calls.append((["semP"], [
+            (own(kp, ci ^ 1, 4), [(at(ci ^ 1, OMAP[kp]), "cin", 2)], "semO", bits(4, 0)),
+            (own(kp, ci ^ 3, 6), [(at(ci ^ 1, SMAP[kp]), "cin", 2)], "semS", bits(4, 4)),
+        ]))
+    calls.append((["semR"], [
+        ([("rowin", s) for s in range(4)], [(at(ci, 4 * (1 - h) + s), "r1", k) for s in range(4)], "r1", bits(16, 0)),
+    ]))
+    ks = inv(SMAP, j)
+    if ks is not None:
+        calls.append((["semS"], [
+            (own(ks, ci ^ 2, 0) + [("cin", 2)], [(at(ci ^ 2, OMAP[ks]), "cin", 3)], "semO", bits(8, 0)),
+        ]))
+    ko = inv(OMAP, j)
+    if ko is not None:
+        calls.append((["semO"], [
+            ([("cin", s) for s in range(4)],
+             [(at(ci, ko), "r2", ci), (at(ci, ko + 4), "r2", ci),
+              (at(ci ^ 2, prim_mate(ko) ^ 4), "r2", ci), (at(ci ^ 1, prim_mate(ko)), "r2", ci)],
+             "c%d" % ci, bits(8, 0)),
+        ]))
+    if j == prim_mate(k):
+        calls.append((["c%d" % (ci ^ 1)], [
+            ([("r2", ci ^ 1)], [(at(ci, j ^ 4), "r2", ci ^ 1), (at(ci ^ 2, j ^ 4), "r2", ci ^ 1)],
+             "c%d" % (ci ^ 1), bits(8, 0)),
+        ]))
+    else:
+        for q in (ci ^ 2, ci ^ 3):
+            calls.append((["c%d" % q], [([("r2", q)], [(at(ci, j ^ 4), "r2", q)], "c%d" % q, bits(16, 0))]))
+    return calls
+
+
+def rank_program(g, core, T, topo):
+    if T.rank_of(core) is None:
+        return
+    total = {}
+    for c in T.cores:
+        for waits, trs in plan(c):
+            for srcs, dsts, sem, mask in trs:
+                n = bin(mask).count("1")
+                for d in dsts:
+                    total[(d[0], sem)] = total.get((d[0], sem), 0) + n
+                total[(c, "sent")] = total.get((c, "sent"), 0) + n
+
+    g.dma_start(T.xs[:], T.x[:]).then_inc(T.sem.ld, 16)
+    g.wait_ge(T.sem.ld, 16)
+
+    g.sync.wait_ge(T.sem.r1, total[(core, "r1")])
+    g.sync.dma_start(T.y1[:], T.r1[:]).then_inc(T.sem.st1, 16)
+    g.sync.wait_ge(T.sem.st1, 16)
+    for s in ("c0", "c1", "c2", "c3"):
+        g.scalar.wait_ge(T.sem[s], total[(core, s)])
+    g.scalar.dma_start(T.y2[:], T.r2[:]).then_inc(T.sem.st2, 16)
+    g.scalar.wait_ge(T.sem.st2, 16)
+
+    for waits, trs in plan(core):
+        for s in waits:
+            g.wait_ge(T.sem[s], total[(core, s)])
+        lst = []
+        for srcs, dsts, sem, mask in trs:
+            ids = []
+            for d in dsts:
+                rid, pid, se = topo.addr(d[0])
+                ids.append(DstId(rid=rid, pnc=pid))
+            lst.append(RemoteDMATransfer(
+                dst_ids=ids, dma_engine_mask=mask, remote_sem=T.sem[sem],
+                srcs=[T[b][s] for b, s in srcs], dsts=[T[d[1]][d[2]] for d in dsts],
+                alu_op=1 if len(srcs) > 1 else 0))
+        g.remote_dma_fused(lst, local_sem=T.sem.sent)
+    g.wait_ge(T.sem.sent, total[(core, "sent")])

@@ -2,29 +2,31 @@ from concourse.bass import DstId, RemoteDMATransfer
 import comms_topo
 
 SCRATCH = {
-    "xs": ("dram", [4, 128, 64], "float32"),
-    "rowin": ("dram", [4, 128, 64], "float32"),
-    "r1": ("dram", [4, 128, 64], "float32"),
-    "cin": ("dram", [8, 128, 64], "float32"),
-    "r2": ("dram", [4, 128, 64], "float32"),
+    "xs": ("dram", [8, 128, 32], "float32"),
+    "gin": ("dram", [8, 128, 32], "float32"),
+    "hin": ("dram", [4, 128, 32], "float32"),
+    "r1": ("dram", [8, 128, 32], "float32"),
+    "r2": ("dram", [8, 128, 32], "float32"),
 }
-SEMAPHORES = ["ld", "st1", "st2", "sent", "semR", "semP", "semS", "semO", "r1", "c0", "c1", "c2", "c3"]
+SEMAPHORES = ["ld", "st1", "st2", "sent", "gs", "hs", "rb", "rs", "cf", "cd"]
 
 FIRST_CHIP = 8
-OMAP = {0: 6, 1: 7, 2: 3, 3: 2}
-SMAP = {0: 0, 1: 1, 2: 4, 3: 5}
-PMAP = {0: 6, 1: 7, 2: 2, 3: 3}
+PLAIN = (0, 1, 4, 5)
+PORT = (2, 3, 6, 7)
 
 
-def inv(m, j):
-    for k in m:
-        if m[k] == j:
-            return k
-    return None
+def handler(ci, e):
+    return PLAIN[e % 4] if e // 4 == ci % 2 else PORT[e % 4]
 
 
-def prim_mate(k):
-    return k + 4 * (k % 2)
+def eighth(ci, j):
+    for e in range(8):
+        if handler(ci, e) == j:
+            return e
+
+
+def helper(k, e):
+    return (2 * k + e // 4) * 8 + PORT[e % 4]
 
 
 def bits(n, at):
@@ -33,64 +35,42 @@ def bits(n, at):
 
 def plan(core):
     chip, j = divmod(core, 8)
+    if chip < FIRST_CHIP:
+        if j not in PORT:
+            return []
+        k, e = chip // 2, 4 * (chip % 2) + PORT.index(j)
+        recv = k + 4 * ((e % 4) // 2)
+        return [(["hs"], [([("hin", c) for c in range(4)],
+                           [((FIRST_CHIP + c) * 8 + recv, "r2", e) for c in range(4)], "cf", bits(8, 0))])]
     ci = chip - FIRST_CHIP
-    k, h = j % 4, j // 4
+    base = chip * 8
+    mine = eighth(ci, j)
 
-    def at(c, jj):
-        return (FIRST_CHIP + c) * 8 + jj
-
-    def own(kk, q, slot0):
-        return [("xs", q) if kk + 4 * hh == j else ("cin", slot0 + hh) for hh in (0, 1)]
+    def copy_of(s):
+        return ("xs", mine) if s == j else ("gin", s)
 
     calls = []
-    tr = []
-    for t in range(4):
-        tr.append(([("xs", t)], [(at(ci, 4 * (1 - h) + t), "rowin", k)], "semR"))
-    tr.append(([("xs", ci)], [(at(ci, OMAP[k]), "cin", h)], "semO"))
-    if SMAP[k] != j:
-        tr.append(([("xs", ci ^ 2)], [(at(ci, SMAP[k]), "cin", h)], "semS"))
-    if PMAP[k] != j:
-        tr.append(([("xs", ci ^ 1)], [(at(ci, PMAP[k]), "cin", 4 + h)], "semP"))
-        tr.append(([("xs", ci ^ 3)], [(at(ci, PMAP[k]), "cin", 6 + h)], "semP"))
+    tr = [([("xs", e)], [(base + handler(ci, e), "gin", j)], "gs") for e in range(8) if e != mine]
     calls.append(([], [t + (bits(2, 2 * i),) for i, t in enumerate(tr)]))
-    kp = inv(PMAP, j)
-    if kp is not None:
-        calls.append((["semP"], [
-            (own(kp, ci ^ 1, 4), [(at(ci ^ 1, OMAP[kp]), "cin", 2)], "semO", bits(4, 0)),
-            (own(kp, ci ^ 3, 6), [(at(ci ^ 1, SMAP[kp]), "cin", 2)], "semS", bits(4, 4)),
-        ]))
-    calls.append((["semR"], [
-        ([("rowin", s) for s in range(4)], [(at(ci, 4 * (1 - h) + s), "r1", k) for s in range(4)], "r1", bits(16, 0)),
-    ]))
-    ks = inv(SMAP, j)
-    if ks is not None:
-        calls.append((["semS"], [
-            (own(ks, ci ^ 2, 0) + [("cin", 2)], [(at(ci ^ 2, OMAP[ks]), "cin", 3)], "semO", bits(8, 0)),
-        ]))
-    ko = inv(OMAP, j)
-    if ko is not None:
-        calls.append((["semO"], [
-            ([("cin", s) for s in range(4)],
-             [(at(ci, ko), "r2", ci), (at(ci, ko + 4), "r2", ci),
-              (at(ci ^ 2, prim_mate(ko) ^ 4), "r2", ci), (at(ci ^ 1, prim_mate(ko)), "r2", ci)],
-             "c%d" % ci, bits(8, 0)),
-        ]))
-    if j == prim_mate(k):
-        calls.append((["c%d" % (ci ^ 1)], [
-            ([("r2", ci ^ 1)], [(at(ci, j ^ 4), "r2", ci ^ 1), (at(ci ^ 2, j ^ 4), "r2", ci ^ 1)],
-             "c%d" % (ci ^ 1), bits(8, 0)),
-        ]))
-    else:
-        for q in (ci ^ 2, ci ^ 3):
-            calls.append((["c%d" % q], [([("r2", q)], [(at(ci, j ^ 4), "r2", q)], "c%d" % q, bits(16, 0))]))
+    tr = [([copy_of(k), copy_of(k + 4)], [(helper(k, mine), "hin", ci)], "hs", bits(2, 2 * k)) for k in range(4)]
+    for d in (0, 1):
+        die = range(4 * d, 4 * d + 4)
+        tr.append(([copy_of(s) for s in die], [(base + s, "r1", mine) for s in die if s != j], "rs", bits(4, 8 + 4 * d)))
+    calls.append((["gs"], tr))
+    e = eighth(ci, j ^ 1)
+    calls.append((["rs"], [([("r1", e)], [(base + (j ^ 1), "r1", e)], "rb", bits(16, 0))]))
+    got = [e for e in range(8) if (e % 4) // 2 == j // 4]
+    calls.append((["cf"], [([("r2", e)], [(base + (j ^ 4), "r2", e)], "cd", bits(4, 4 * i))
+                           for i, e in enumerate(got)]))
     return calls
 
 
 def rank_program(g, core, T, topo):
-    if T.rank_of(core) is None:
+    calls = plan(core)
+    if not calls:
         return
     total = {}
-    for c in T.cores:
+    for c in range((FIRST_CHIP + 4) * 8):
         for waits, trs in plan(c):
             for srcs, dsts, sem, mask in trs:
                 n = bin(mask).count("1")
@@ -98,18 +78,17 @@ def rank_program(g, core, T, topo):
                     total[(d[0], sem)] = total.get((d[0], sem), 0) + n
                 total[(c, "sent")] = total.get((c, "sent"), 0) + n
 
-    g.dma_start(T.xs[:], T.x[:]).then_inc(T.sem.ld, 16)
-    g.wait_ge(T.sem.ld, 16)
+    if T.rank_of(core) is not None:
+        g.dma_start(T.xs[:], T.x[:]).then_inc(T.sem.ld, 16)
+        g.wait_ge(T.sem.ld, 16)
+        for q, sems, y, r, st in ((g.sync, ("rb", "rs"), T.y1, T.r1, T.sem.st1),
+                                  (g.scalar, ("cf", "cd"), T.y2, T.r2, T.sem.st2)):
+            for s in sems:
+                q.wait_ge(T.sem[s], total[(core, s)])
+            q.dma_start(y[:], r[:]).then_inc(st, 16)
+            q.wait_ge(st, 16)
 
-    g.sync.wait_ge(T.sem.r1, total[(core, "r1")])
-    g.sync.dma_start(T.y1[:], T.r1[:]).then_inc(T.sem.st1, 16)
-    g.sync.wait_ge(T.sem.st1, 16)
-    for s in ("c0", "c1", "c2", "c3"):
-        g.scalar.wait_ge(T.sem[s], total[(core, s)])
-    g.scalar.dma_start(T.y2[:], T.r2[:]).then_inc(T.sem.st2, 16)
-    g.scalar.wait_ge(T.sem.st2, 16)
-
-    for waits, trs in plan(core):
+    for waits, trs in calls:
         for s in waits:
             g.wait_ge(T.sem[s], total[(core, s)])
         lst = []

@@ -79,7 +79,7 @@ def rank_program(g, core, T, topo):
                 total[(c, "sent")] = total.get((c, "sent"), 0) + n
 
     if T.rank_of(core) is not None:
-        g.dma_start(T.xs[:], T.x[:]).then_inc(T.sem.ld, 16)
+        g.sync.dma_start(T.xs[:], T.x[:]).then_inc(T.sem.ld, 16)
         g.wait_ge(T.sem.ld, 16)
         for q, sems, y, r, st in ((g.sync, ("rb", "rs"), T.y1, T.r1, T.sem.st1),
                                   (g.scalar, ("cf", "cd"), T.y2, T.r2, T.sem.st2)):

from concourse.bass import DstId, RemoteDMATransfer
import comms_topo

SCRATCH = {
    "xs": ("dram", [8, 128, 32], "float32"),
    "gin": ("dram", [8, 128, 32], "float32"),
    "hin": ("dram", [4, 128, 32], "float32"),
    "r1": ("dram", [8, 128, 32], "float32"),
    "r2": ("dram", [8, 128, 32], "float32"),
}
SEMAPHORES = ["ld", "st1", "st2", "sent", "gs", "hs", "rb", "rs", "cf", "cd"]

FIRST_CHIP = 8
PLAIN = (0, 1, 4, 5)
PORT = (2, 3, 6, 7)


def handler(ci, e):
    return PLAIN[e % 4] if e // 4 == ci % 2 else PORT[e % 4]


def eighth(ci, j):
    for e in range(8):
        if handler(ci, e) == j:
            return e


def helper(k, e):
    return (2 * k + e // 4) * 8 + PORT[e % 4]


def bits(n, at):
    return ((1 << n) - 1) << at


def plan(core):
    chip, j = divmod(core, 8)
    if chip < FIRST_CHIP:
        if j not in PORT:
            return []
        k, e = chip // 2, 4 * (chip % 2) + PORT.index(j)
        recv = k + 4 * ((e % 4) // 2)
        return [(["hs"], [([("hin", c) for c in range(4)],
                           [((FIRST_CHIP + c) * 8 + recv, "r2", e) for c in range(4)], "cf", bits(8, 0))])]
    ci = chip - FIRST_CHIP
    base = chip * 8
    mine = eighth(ci, j)

    def copy_of(s):
        return ("xs", mine) if s == j else ("gin", s)

    calls = []
    tr = [([("xs", e)], [(base + handler(ci, e), "gin", j)], "gs") for e in range(8) if e != mine]
    calls.append(([], [t + (bits(2, 2 * i),) for i, t in enumerate(tr)]))
    tr = [([copy_of(k), copy_of(k + 4)], [(helper(k, mine), "hin", ci)], "hs", bits(2, 2 * k)) for k in range(4)]
    for d in (0, 1):
        die = range(4 * d, 4 * d + 4)
        tr.append(([copy_of(s) for s in die], [(base + s, "r1", mine) for s in die if s != j], "rs", bits(4, 8 + 4 * d)))
    calls.append((["gs"], tr))
    e = eighth(ci, j ^ 1)
    calls.append((["rs"], [([("r1", e)], [(base + (j ^ 1), "r1", e)], "rb", bits(16, 0))]))
    got = [e for e in range(8) if (e % 4) // 2 == j // 4]
    calls.append((["cf"], [([("r2", e)], [(base + (j ^ 4), "r2", e)], "cd", bits(4, 4 * i))
                           for i, e in enumerate(got)]))
    return calls


def rank_program(g, core, T, topo):
    calls = plan(core)
    if not calls:
        return
    total = {}
    for c in range((FIRST_CHIP + 4) * 8):
        for waits, trs in plan(c):
            for srcs, dsts, sem, mask in trs:
                n = bin(mask).count("1")
                for d in dsts:
                    total[(d[0], sem)] = total.get((d[0], sem), 0) + n
                total[(c, "sent")] = total.get((c, "sent"), 0) + n

    if T.rank_of(core) is not None:
        g.sync.dma_start(T.xs[:], T.x[:]).then_inc(T.sem.ld, 16)
        g.wait_ge(T.sem.ld, 16)
        for q, sems, y, r, st in ((g.sync, ("rb", "rs"), T.y1, T.r1, T.sem.st1),
                                  (g.scalar, ("cf", "cd"), T.y2, T.r2, T.sem.st2)):
            for s in sems:
                q.wait_ge(T.sem[s], total[(core, s)])
            q.dma_start(y[:], r[:]).then_inc(st, 16)
            q.wait_ge(st, 16)

    for waits, trs in calls:
        for s in waits:
            g.wait_ge(T.sem[s], total[(core, s)])
        lst = []
        for srcs, dsts, sem, mask in trs:
            ids = []
            for d in dsts:
                rid, pid, se = topo.addr(d[0])
                ids.append(DstId(rid=rid, pnc=pid))
            lst.append(RemoteDMATransfer(
                dst_ids=ids, dma_engine_mask=mask, remote_sem=T.sem[sem],
                srcs=[T[b][s] for b, s in srcs], dsts=[T[d[1]][d[2]] for d in dsts],
                alu_op=1 if len(srcs) > 1 else 0))
        g.remote_dma_fused(lst, local_sem=T.sem.sent)
    g.wait_ge(T.sem.sent, total[(core, "sent")])
